import numpy as np
import ml_dtypes


def mxq(x, axis, fmt="e4m3"):
    dtype, down = {"e4m3": (ml_dtypes.float8_e4m3fn, 7), "e5m2": (ml_dtypes.float8_e5m2, 14)}[fmt]
    v = np.moveaxis(np.asarray(x, np.float32).astype(ml_dtypes.bfloat16).astype(np.float64), axis, -1)
    blocks = v.reshape(v.shape[:-1] + (-1, 32))
    amax = np.abs(blocks).max(-1, keepdims=True)
    byte = np.maximum(np.where(amax > 0, np.frexp(amax)[1] - 1 + 127, 0) - down, 1)
    scale = np.exp2(byte - 127.0)
    codes = (blocks / scale).astype(np.float32).astype(dtype).astype(np.float64)
    return np.moveaxis((codes * scale).reshape(v.shape), -1, axis)


WIDE = False


def mx_kscale(k):
    if not WIDE:
        return np.ones(k)
    levels = np.array([10, -10, 5, -5, 0])
    if k % 512:
        return np.exp2(np.random.permutation(np.resize(levels, k // 32))).repeat(32)
    a = np.empty((k // 512, 16))
    for p in range(k // 512):
        a[p, :8] = np.random.permutation(np.resize(levels, 8))
        for g in range(8):
            far = levels[np.abs(levels - a[p, g]) >= 10]
            a[p, g + 8] = far[np.random.randint(len(far))]
    return np.exp2(a.ravel()).repeat(32)


BF16 = ml_dtypes.bfloat16


def bf(x):
    return np.asarray(x, np.float32).astype(BF16)


def f64(x):
    return np.asarray(x).astype(np.float64)


E2M1 = np.array([0.0, 0.5, 1.0, 1.5, 2.0, 3.0, 4.0, 6.0, -0.0, -0.5, -1.0, -1.5, -2.0, -3.0, -4.0, -6.0])


def pack_weight(w, fmt):
    k, n = w.shape
    w = f64(bf(w)).reshape(k // 32, 32, n)
    amax = np.abs(w).max(1)
    if fmt == "e4m3":
        byte = np.frexp(amax)[1] - 1 + 127 - 7
    else:
        mant, ex = np.frexp(amax / 6.0)
        byte = np.where(mant > 0.5, ex, ex - 1) + 127
    byte = np.clip(np.where(amax > 0, byte, 1), 1, 254)
    scaled = (w * np.exp2(127.0 - byte)[:, None, :]).reshape(k, n).astype(np.float32)
    by_word = np.ascontiguousarray(scaled.reshape(k // 512, 128, 4, n).transpose(0, 1, 3, 2))
    if fmt == "e4m3":
        words = by_word.astype(ml_dtypes.float8_e4m3fn).view(np.uint8)
    else:
        c = by_word.astype(ml_dtypes.float4_e2m1fn).view(np.uint8) & 0xF
        words = c[..., 0::2] | (c[..., 1::2] << 4)
    return np.ascontiguousarray(words), np.ascontiguousarray(byte.astype(np.uint8).reshape(k // 512, 16, n))


def unpack_weight(words, scales, fmt):
    g, p, n, _ = words.shape
    if fmt == "e4m3":
        vals = np.ascontiguousarray(words).view(ml_dtypes.float8_e4m3fn).astype(np.float64)
    else:
        nib = np.empty((g, p, n, 4), np.uint8)
        nib[..., 0::2] = words & 0xF
        nib[..., 1::2] = words >> 4
        vals = E2M1[nib]
    vals = vals * np.repeat(np.exp2(scales.astype(np.float64) - 127.0), 8, axis=1)[..., None]
    return vals.transpose(0, 1, 3, 2).reshape(g * 512, n)
def pack4(w):
    words, scales = pack_weight(w, "e2m1")
    return words.reshape(words.shape[0], 128, -1), scales


def unpack4(words, scales):
    return unpack_weight(words.reshape(words.shape[0], 128, -1, 2), scales, "e2m1")


def planes(Y):
    n, m = Y.shape
    b = f64(bf(Y)).reshape(n // 32, 32, m)
    amax = np.abs(b).max(1)
    byte = np.clip(np.where(amax > 0, np.frexp(amax)[1] - 1 + 127 - 7, 1), 1, 254)
    codes = (b * np.exp2(127.0 - byte)[:, None, :]).reshape(n, m).astype(np.float32).astype(ml_dtypes.float8_e4m3fn).view(np.uint8)
    words = codes.reshape(n // 512, 128, 4, m).transpose(0, 1, 3, 2)
    return np.ascontiguousarray(words), np.ascontiguousarray(byte.astype(np.uint8).reshape(n // 512, 16, m))


R, C, D, P = 2048, 4, 512, 2
K = C * D


def setup_inputs():
    t = mx_kscale(K)
    h0 = bf(np.random.standard_normal((R, D)))
    dx = bf(np.random.standard_normal((P, R, C)))
    words, scales = pack4(np.random.standard_normal((K, D)) / np.sqrt(K) / t[:, None])
    return {"h0": h0,
            "dx": dx,
            "a_words": words,
            "a_scales": scales,
            "gain": bf((1.0 + 0.1 * np.random.standard_normal((C, D))) * t.reshape(C, D)),
            "b": bf(np.random.standard_normal((C, D)) * 0.3)}


def euler_step(h, dx_t, aq, gain, b):
    z = dx_t[:, :, None] * gain[None, :, :] * h[:, None, :]
    z = z.reshape(h.shape[0], K)
    return h + (mxq(z, 1, "e4m3") @ aq) + np.sum(dx_t[:, :, None] * b[None, :, :], axis=1)


def core(h0, dx, a_words, a_scales, gain, b):
    h, d, g, bias = f64(h0), f64(dx), f64(gain), f64(b)
    aq = unpack4(a_words, a_scales)
    h1 = euler_step(h, d[0], aq, g, bias)
    h2 = euler_step(h1, d[1], aq, g, bias)
    return h2


def reference(h0, dx, a_words, a_scales, gain, b):
    R_out = core(h0, dx, a_words, a_scales, gain, b)
    words, scales = planes(R_out.T)
    return R_out, words, scales

@@ -1,0 +1,300 @@
+from contextlib import ExitStack
+
+import concourse.mybir as mybir
+from concourse.masks import make_identity
+
+R, C, D = 2048, 4, 512
+K = C * D
+FLOPS = 2 * 2 * R * K * D
+
+F32 = mybir.dt.float32
+BF16 = mybir.dt.bfloat16
+I32 = mybir.dt.int32
+U32 = mybir.dt.uint32
+U8 = mybir.dt.uint8
+FP8X4 = mybir.dt.float8_e4m3fn_x4
+FP4X4 = mybir.dt.float4_e2m1fn_x4
+MULT = mybir.AluOpType.mult
+ADD = mybir.AluOpType.add
+COPY = mybir.ActivationFunctionType.Copy
+AX = mybir.AxisListType
+
+P = 128
+TILES = R // P
+G = 4
+
+
+def perm(ap):
+    return ap.rearrange("k (p u e) -> k u p e", u=2, e=2)
+
+
+def lin(ap):
+    return ap.rearrange("k (u p e) -> k u p e", u=2, e=2)
+
+
+def unperm(ap):
+    return ap.rearrange("k (u p e) -> k p u e", u=2, e=2)
+
+
+def nat(ap):
+    return ap.rearrange("k (p u e) -> k p u e", u=2, e=2)
+
+
+def tile_linearneuralcdetwoeulersteps_x2_kernel(tc, h0, dx, a_words, a_scales, gain, b, out_0, out_1, out_2):
+    nc = tc.nc
+    with ExitStack() as ctx:
+        keep = ctx.enter_context(tc.tile_pool(name="keep", bufs=1))
+        work = ctx.enter_context(tc.tile_pool(name="work", bufs=3))
+        psk = ctx.enter_context(tc.psum_pool(name="psk", bufs=1))
+        ps = ctx.enter_context(tc.psum_pool(name="ps", bufs=2))
+        ctx.enter_context(tc.manual_schedule())
+
+        h0_v = h0.rearrange("(g p j) d -> g p j d", g=4, j=4)
+        out_v = out_0.rearrange("(g p j) d -> g p j d", g=4, j=4)
+        dx_v = dx.rearrange("s (g p j) c -> s p g (j c)", g=4, j=4)
+
+        h_in = [keep.tile([P, G, D], BF16, name="h_in%d" % g, align_bytes=64) for g in range(4)]
+        e_bf = keep.tile([P, 2, 4, 16], BF16, name="e_bf")
+        e_f = keep.tile([P, 128], F32, name="e_f")
+        e_t = keep.tile([P, 128], BF16, name="e_t")
+        gain_row = keep.tile([P, K], BF16, name="gain_row", align_bytes=64)
+        ones_row = keep.tile([P, P], BF16, name="ones_row", align_bytes=64)
+        gain_sb = keep.tile([P, K], BF16, name="gain_sb", align_bytes=64)
+        b_rep = keep.tile([P, D], BF16, name="b_rep", align_bytes=64)
+        aw = keep.tile([P, 4, 2 * D], U8, name="aw", align_bytes=64)
+        asc = keep.tile([P, 4, D], U8, name="asc", align_bytes=64)
+        id_f = keep.tile([P, P], F32, name="id_f", align_bytes=64)
+        id_b = keep.tile([P, P], BF16, name="id_b", align_bytes=64)
+        sel = keep.tile([P, 32], F32, name="sel")
+        gain_ps = [psk.tile([P, 1024], BF16, name="gain_ps%d" % i) for i in range(2)]
+
+        nc.vector.memset(gain_row[:], 0.0)
+        nc.vector.memset(ones_row[:], 0.0)
+        nc.vector.memset(ones_row[0:1, :], 1.0)
+        nc.vector.memset(asc[:].rearrange("p g n -> p (g n)").bitcast(I32), 0)
+        make_identity(nc, id_f[:])
+
+        nc.scalar.dma_start(out=gain_row[0:1, :], in_=gain.rearrange("(o c) d -> o (c d)", o=1))
+        nc.sync.dma_start(out=h_in[0][:, 0:1, :], in_=h0_v[0][:, 0:1, :])
+        for s in range(2):
+            nc.sync.dma_start(out=e_bf[:, s], in_=dx_v[s])
+        nc.sync.dma_start(out=h_in[0][:, 1:4, :], in_=h0_v[0][:, 1:4, :])
+        for c in range(C):
+            nc.scalar.dma_start(out=b_rep[c:P:4, :], in_=b[c : c + 1, :].to_broadcast([32, D]))
+        nc.sync.dma_start(
+            out=aw[:].bitcast(I32), in_=a_words.bitcast(I32).rearrange("g p n -> p g n"))
+        for q in range(4):
+            nc.sync.dma_start(
+                out=asc[32 * q : 32 * q + 4].bitcast(I32),
+                in_=a_scales.bitcast(I32).rearrange("g q n -> q g n")[4 * q : 4 * q + 4])
+        for g in range(1, 4):
+            nc.sync.dma_start(out=h_in[g][:], in_=h0_v[g])
+
+        nc.vector.tensor_copy(out=id_b[:], in_=id_f[:])
+        nc.vector.tensor_reduce(out=sel[:], in_=id_f[:].rearrange("k (i c) -> k i c", c=4), op=ADD, axis=AX.X)
+        for c in range(C):
+            nc.tensor.matmul(lin(gain_ps[c // 2][:, (c % 2) * D : (c % 2 + 1) * D]), lhsT=ones_row[:],
+                             rhs=perm(gain_row[:, c * D : (c + 1) * D]), start=True, stop=True)
+        nc.scalar.activation(out=e_f[:], in_=e_bf[:].rearrange("p s g x -> p (s g x)"), func=COPY)
+        et_ps = ps.tile([P, P], BF16, name="et_ps", tag="tr")
+        nc.tensor.transpose(et_ps[:], e_bf[:].rearrange("p s g x -> p (s g x)"), id_b[:])
+        nc.vector.tensor_copy(out=e_t[:], in_=et_ps[:])
+        for c in range(C):
+            nc.scalar.copy(out=nat(gain_sb[:, c * D : (c + 1) * D]),
+                           in_=unperm(gain_ps[c // 2][:, (c % 2) * D : (c % 2 + 1) * D]))
+
+        st = {}
+
+        def new(key, t, shape, dt, bufs, **kw):
+            x = work.tile(shape, dt, name=key, bufs=bufs, align_bytes=64)
+            st[(key, t)] = x
+            return x
+
+        def hrow(t):
+            return h_in[t // G][:, t % G, :]
+
+        def ecol(s, t, c):
+            i = (s * TILES + t) * 4 + c
+            return e_f[:, i : i + 1]
+
+        def gps(c):
+            return gain_ps[c // 2][:, (c % 2) * D : (c % 2 + 1) * D]
+
+        def v_set(t):
+            return (0, 1, 2, 3) if t == 0 else (0,)
+
+        def g_u(t):
+            for c in range(C):
+                if c not in v_set(t):
+                    u = new("u%d" % c, t, [P, D], F32, 2)
+                    nc.gpsimd.tensor_tensor(out=u[:], in0=hrow(t), in1=gain_sb[:, c * D : (c + 1) * D], op=MULT)
+
+        def v_z1(t):
+            z = new("z1", t, [P, K], BF16, 3)
+            for c in v_set(t):
+                for u in range(2):
+                    nc.vector.scalar_tensor_tensor(
+                        out=z[:, c * D + 256 * u : c * D + 256 * (u + 1)].rearrange("k (p e) -> k p e", e=2),
+                        in0=perm(hrow(t))[:, u], scalar=ecol(0, t, c),
+                        in1=gps(c)[:, 256 * u : 256 * (u + 1)].rearrange("k (p e) -> k p e", e=2), op0=MULT, op1=MULT)
+
+        def s_z1(t):
+            z = st[("z1", t)]
+            for c in range(C):
+                if c not in v_set(t):
+                    nc.scalar.activation(out=lin(z[:, c * D : (c + 1) * D]), in_=perm(st[("u%d" % c, t)][:]), func=COPY,
+                                         scale=ecol(0, t, c))
+
+        def v_mask(s, t):
+            m = new("m%d" % s, t, [P, P], BF16, 3)
+            i = s * TILES + t
+            nc.vector.tensor_scalar(out=m[:], in0=e_t[:], scalar1=sel[:, i : i + 1], scalar2=None, op0=MULT)
+
+        def t_p(t):
+            eb = ps.tile([P, D], F32, name="eb", tag="eb")
+            st[("p", t)] = eb
+            nc.tensor.matmul(eb[:], lhsT=st[("m0", t)][:], rhs=b_rep[:], start=True, stop=(t == 0))
+            if t > 0:
+                nc.tensor.matmul(eb[:], lhsT=id_b[:], rhs=hrow(t), start=False, stop=True)
+
+        def s_p(t):
+            p = new("ph", t, [P, D], F32, 2)
+            src = st[("p", t)]
+            if t == 0:
+                nc.vector.tensor_tensor(out=lin(p[:]), in0=perm(src[:]), in1=perm(hrow(t)), op=ADD)
+            else:
+                nc.scalar.copy(out=lin(p[:]), in_=perm(src[:]))
+
+        def t_tr(key, t, half):
+            b_ = ps.tile([P, 4, P], F32, name="tr", tag="tr")
+            st[("tr", key, t, half)] = b_
+            w = st[(key, t)][:].bitcast(F32)
+            for i in range(4):
+                n = half * 4 + i
+                nc.tensor.transpose(b_[:, i, :], w[:, n * P : (n + 1) * P], id_f[:])
+
+        def s_cp(key, t, half):
+            if half == 0:
+                new(key + "t", t, [P, K], BF16, 2)
+            dst = st[(key + "t", t)][:, half * 1024 : (half + 1) * 1024].bitcast(F32)
+            nc.scalar.copy(out=dst.rearrange("p (c r u) -> p c r u", c=2, u=2),
+                           in_=st[("tr", key, t, half)][:].rearrange("p (c u) r -> p c r u", c=2))
+
+        def v_q(key, t):
+            codes = new(key + "c", t, [P, D], U32, 2)
+            sc = new(key + "s", t, [P, D], U8, 2)
+            nc.vector.quantize_mx(out=codes[:].bitcast(FP8X4), scales=sc[:], in_=st[(key + "t", t)][:])
+
+        def t_mx(key, t):
+            acc = ps.tile([P, D], F32, name="mx", tag="mx")
+            st[("mx", key, t)] = acc
+            codes, sc = st[(key + "c", t)], st[(key + "s", t)]
+            for c in range(C):
+                nc.tensor.matmul_mx(
+                    out=acc[:], lhsT=codes[:, c * P : (c + 1) * P].bitcast(FP8X4), lhsT_scale=sc[:, c * P : (c + 1) * P],
+                    rhs=aw[:, c, :].bitcast(FP4X4), rhs_scale=asc[:, c, :], start=(c == 0), stop=(c == C - 1))
+
+        def v_h1(t):
+            h = new("h1", t, [P, D], F32, 3)
+            nc.vector.tensor_tensor(out=lin(h[:]), in0=perm(st[("mx", "z1", t)][:]), in1=lin(st[("ph", t)][:]), op=ADD)
+
+        def v_z2(t):
+            z = new("z2", t, [P, K], BF16, 2)
+            for c in range(C):
+                nc.vector.scalar_tensor_tensor(out=z[:, c * D : (c + 1) * D], in0=st[("h1", t)][:], scalar=ecol(1, t, c),
+                                               in1=gps(c), op0=MULT, op1=MULT)
+
+        def t_eb(t):
+            eb = ps.tile([P, D], F32, name="eb", tag="eb")
+            st[("eb", t)] = eb
+            nc.tensor.matmul(eb[:], lhsT=st[("m1", t)][:], rhs=b_rep[:], start=True, stop=True)
+
+        def v_w(t):
+            w = new("w", t, [P, D], F32, 2)
+            nc.vector.tensor_tensor(out=nat(w[:]), in0=unperm(st[("h1", t)][:]), in1=nat(st[("eb", t)][:]), op=ADD)
+
+        def v_out(t):
+            o = new("o", t, [P, D], F32, 3)
+            nc.vector.tensor_tensor(out=o[:], in0=st[("mx", "z2", t)][:], in1=st[("w", t)][:], op=ADD)
+            nc.sync.dma_start(out=out_v[t // G][:, t % G, :], in_=o[:])
+
+        def s_ob(t):
+            ob = new("ob", t, [P, D], BF16, 3)
+            nc.scalar.copy(out=lin(ob[:]), in_=perm(st[("o", t)][:]))
+
+        def t_trp(t):
+            b_ = ps.tile([P, 4, P], F32, name="tr", tag="tr")
+            st[("trp", t)] = b_
+            for jj in range(2):
+                w = st[("ob", t - 1 + jj)][:].bitcast(F32)
+                for u in range(2):
+                    nc.tensor.transpose(b_[:, 2 * jj + u, :], w[:, u * P : (u + 1) * P], id_f[:])
+
+        def s_cpp(t):
+            g = t // G
+            if t % G == 1:
+                new("pt", g, [P, K], BF16, 2)
+            dst = st[("pt", g)][:].bitcast(F32).rearrange("p (q j u) -> p q j u", j=4, u=2)
+            h = (t % G) // 2
+            nc.scalar.copy(out=dst[:, :, 2 * h : 2 * h + 2, :],
+                           in_=st[("trp", t)][:].rearrange("p (j u) q -> p q j u", u=2))
+
+        def v_planes(g):
+            codes = new("pc", g, [P, D], U32, 2)
+            sc = new("psc", g, [P, D], U8, 2)
+            nc.vector.quantize_mx(out=codes[:].bitcast(FP8X4), scales=sc[:], in_=st[("pt", g)][:])
+            dst = out_1.rearrange("o p m t -> (o p) (m t)")
+            nc.sync.dma_start(out=dst[:, g * K : (g + 1) * K].bitcast(I32), in_=codes[:].bitcast(I32))
+            dst2 = out_2.rearrange("o q m -> (o q) m")
+            for q in range(4):
+                nc.sync.dma_start(out=dst2[4 * q : 4 * q + 4, g * D : (g + 1) * D].bitcast(I32),
+                                  in_=sc[32 * q : 32 * q + 4, :].bitcast(I32))
+
+        def ok(t):
+            return 0 <= t < TILES
+
+        for k in range(-2, TILES + 4):
+            if ok(k + 2):
+                g_u(k + 2)
+            if ok(k + 1):
+                s_z1(k + 1)
+                t_p(k + 1)
+                s_p(k + 1)
+            if ok(k - 2):
+                v_q("z2", k - 2)
+                t_mx("z2", k - 2)
+            if ok(k):
+                v_q("z1", k)
+                t_mx("z1", k)
+            if ok(k - 1):
+                v_z2(k - 1)
+                t_tr("z2", k - 1, 0)
+                s_cp("z2", k - 1, 0)
+            if ok(k - 2):
+                v_out(k - 2)
+            if ok(k + 1):
+                t_tr("z1", k + 1, 0)
+                s_cp("z1", k + 1, 0)
+                t_tr("z1", k + 1, 1)
+                s_cp("z1", k + 1, 1)
+            if ok(k + 2):
+                v_z1(k + 2)
+            if ok(k - 1):
+                t_tr("z2", k - 1, 1)
+                s_cp("z2", k - 1, 1)
+                t_eb(k - 1)
+            if ok(k):
+                v_h1(k)
+            if ok(k - 1):
+                v_w(k - 1)
+            if ok(k - 2):
+                s_ob(k - 2)
+                if (k - 2) % 2 == 1:
+                    t_trp(k - 2)
+                    s_cpp(k - 2)
+            if ok(k - 3) and (k - 3) % G == 3:
+                v_planes((k - 3) // G)
+            if ok(k + 2):
+                v_mask(0, k + 2)
+            if ok(k):
+                v_mask(1, k)

@@ -22,6 +22,17 @@ AX = mybir.AxisListType
 P = 128
 TILES = R // P
 G = 4
+BUFS = {"pt":2,"pc":2,"psc":2,"m0":2,"m1":5,"ph":6,"z1t":5,"z2t":2,"z1c":2,"z1s":2,"z2c":2,"z2s":2,"h1":4,"w":3,"o":3,"z1":5,"z2":2,"ob":5}
+NTR, NMX, NEB = 2, 2, 2
+G1 = ()
+G2 = ()
+G2X = {}
+SEQ = [
+    ("trp", 1), ("q1", -6), ("tr1b", -7), ("q2", -3), ("h1", -5), ("w", -3), ("cP", -10), ("tr2a", -4),
+    ("tr2b", -4), ("c1a", -10), ("out", -2), ("m1", -7), ("eb", -4), ("z12", -9), ("mx1", -6), ("pq", 2),
+    ("cpp", 1), ("c2a", -4), ("z20", -5), ("P", -11), ("z21", -5), ("mx2", -3), ("m0", -12), ("z22", -5),
+    ("z11", -11), ("z10", -11), ("c1b", -7), ("tr1a", -11), ("z23", -5), ("c2b", -4), ("z13", -8), ("ob", -2),
+]
 
 
 def perm(ap):
@@ -59,6 +70,7 @@ def tile_linearneuralcdetwoeulersteps_x2_kernel(tc, h0, dx, a_words, a_scales, g
         e_t = keep.tile([P, 128], BF16, name="e_t")
         gain_row = keep.tile([P, K], BF16, name="gain_row", align_bytes=64)
         ones_row = keep.tile([P, P], BF16, name="ones_row", align_bytes=64)
+        gain_f = keep.tile([P, K], F32, name="gain_f", align_bytes=64)
         gain_sb = keep.tile([P, K], BF16, name="gain_sb", align_bytes=64)
         b_rep = keep.tile([P, D], BF16, name="b_rep", align_bytes=64)
         aw = keep.tile([P, 4, 2 * D], U8, name="aw", align_bytes=64)
@@ -100,15 +112,20 @@ def tile_linearneuralcdetwoeulersteps_x2_kernel(tc, h0, dx, a_words, a_scales, g
         nc.tensor.transpose(et_ps[:], e_bf[:].rearrange("p s g x -> p (s g x)"), id_b[:])
         nc.vector.tensor_copy(out=e_t[:], in_=et_ps[:])
         for c in range(C):
-            nc.scalar.copy(out=nat(gain_sb[:, c * D : (c + 1) * D]),
-                           in_=unperm(gain_ps[c // 2][:, (c % 2) * D : (c % 2 + 1) * D]))
+            if c in G1:
+                nc.scalar.copy(out=nat(gain_sb[:, c * D : (c + 1) * D]),
+                               in_=unperm(gain_ps[c // 2][:, (c % 2) * D : (c % 2 + 1) * D]))
+        for c in range(C):
+            if c in G2:
+                nc.scalar.copy(out=gain_f[:, c * D : (c + 1) * D], in_=gain_ps[c // 2][:, (c % 2) * D : (c % 2 + 1) * D])
 
         st = {}
 
-        def new(key, t, shape, dt, bufs, **kw):
-            x = work.tile(shape, dt, name=key, bufs=bufs, align_bytes=64)
-            st[(key, t)] = x
-            return x
+        def new(key, t, shape, dt):
+            if (key, t) not in st:
+                x = work.tile(shape, dt, name=key, bufs=BUFS[key], align_bytes=64)
+                st[(key, t)] = x
+            return st[(key, t)]
 
         def hrow(t):
             return h_in[t // G][:, t % G, :]
@@ -120,73 +137,91 @@ def tile_linearneuralcdetwoeulersteps_x2_kernel(tc, h0, dx, a_words, a_scales, g
         def gps(c):
             return gain_ps[c // 2][:, (c % 2) * D : (c % 2 + 1) * D]
 
-        def v_set(t):
-            return (0, 1, 2, 3) if t == 0 else (0,)
+        def g1(t):
+            return () if t == 0 else G1
 
-        def g_u(t):
-            for c in range(C):
-                if c not in v_set(t):
-                    u = new("u%d" % c, t, [P, D], F32, 2)
-                    nc.gpsimd.tensor_tensor(out=u[:], in0=hrow(t), in1=gain_sb[:, c * D : (c + 1) * D], op=MULT)
+        def g2(t):
+            return G2X.get(t, G2)
 
-        def v_z1(t):
-            z = new("z1", t, [P, K], BF16, 3)
-            for c in v_set(t):
-                for u in range(2):
-                    nc.vector.scalar_tensor_tensor(
-                        out=z[:, c * D + 256 * u : c * D + 256 * (u + 1)].rearrange("k (p e) -> k p e", e=2),
-                        in0=perm(hrow(t))[:, u], scalar=ecol(0, t, c),
-                        in1=gps(c)[:, 256 * u : 256 * (u + 1)].rearrange("k (p e) -> k p e", e=2), op0=MULT, op1=MULT)
+        def z1(t, c):
+            if c in g1(t):
+                return
+            z = new("z1", t, [P, K], BF16)
+            for u in range(2):
+                nc.vector.scalar_tensor_tensor(
+                    out=z[:, c * D + 256 * u : c * D + 256 * (u + 1)].rearrange("k (p e) -> k p e", e=2),
+                    in0=perm(hrow(t))[:, u], scalar=ecol(0, t, c),
+                    in1=gps(c)[:, 256 * u : 256 * (u + 1)].rearrange("k (p e) -> k p e", e=2), op0=MULT, op1=MULT)
 
-        def s_z1(t):
-            z = st[("z1", t)]
-            for c in range(C):
-                if c not in v_set(t):
-                    nc.scalar.activation(out=lin(z[:, c * D : (c + 1) * D]), in_=perm(st[("u%d" % c, t)][:]), func=COPY,
-                                         scale=ecol(0, t, c))
+        def u1(t, c):
+            if c in g1(t):
+                u = new("u1%d" % c, t, [P, D], F32)
+                nc.gpsimd.tensor_tensor(out=u[:], in0=hrow(t), in1=gain_sb[:, c * D : (c + 1) * D], op=MULT)
 
-        def v_mask(s, t):
-            m = new("m%d" % s, t, [P, P], BF16, 3)
+        def a1(t, c):
+            if c in g1(t):
+                z = new("z1", t, [P, K], BF16)
+                nc.scalar.activation(out=lin(z[:, c * D : (c + 1) * D]), in_=perm(st[("u1%d" % c, t)][:]), func=COPY,
+                                     scale=ecol(0, t, c))
+
+        def z2(t, c):
+            if c in g2(t):
+                return
+            z = new("z2", t, [P, K], BF16)
+            nc.vector.scalar_tensor_tensor(out=z[:, c * D : (c + 1) * D], in0=st[("h1", t)][:], scalar=ecol(1, t, c),
+                                           in1=gps(c), op0=MULT, op1=MULT)
+
+        def u2(t, c):
+            if c in g2(t):
+                u = new("u2%d" % c, t, [P, D], F32)
+                nc.gpsimd.tensor_tensor(out=u[:], in0=st[("h1", t)][:], in1=gain_f[:, c * D : (c + 1) * D], op=MULT)
+
+        def a2(t, c):
+            if c in g2(t):
+                z = new("z2", t, [P, K], BF16)
+                nc.scalar.activation(out=z[:, c * D : (c + 1) * D], in_=st[("u2%d" % c, t)][:], func=COPY,
+                                     scale=ecol(1, t, c))
+
+        def mask(t, s):
+            m = new("m%d" % s, t, [P, P], BF16)
             i = s * TILES + t
             nc.vector.tensor_scalar(out=m[:], in0=e_t[:], scalar1=sel[:, i : i + 1], scalar2=None, op0=MULT)
 
-        def t_p(t):
-            eb = ps.tile([P, D], F32, name="eb", tag="eb")
+        def p_mm(t):
+            eb = ps.tile([P, D], F32, name="eb", tag="eb", bufs=NEB)
             st[("p", t)] = eb
             nc.tensor.matmul(eb[:], lhsT=st[("m0", t)][:], rhs=b_rep[:], start=True, stop=(t == 0))
             if t > 0:
                 nc.tensor.matmul(eb[:], lhsT=id_b[:], rhs=hrow(t), start=False, stop=True)
 
-        def s_p(t):
-            p = new("ph", t, [P, D], F32, 2)
+        def p_cp(t):
+            p = new("ph", t, [P, D], F32)
             src = st[("p", t)]
             if t == 0:
                 nc.vector.tensor_tensor(out=lin(p[:]), in0=perm(src[:]), in1=perm(hrow(t)), op=ADD)
             else:
                 nc.scalar.copy(out=lin(p[:]), in_=perm(src[:]))
 
-        def t_tr(key, t, half):
-            b_ = ps.tile([P, 4, P], F32, name="tr", tag="tr")
+        def tr(t, key, half):
+            b_ = ps.tile([P, 4, P], F32, name="tr", tag="tr", bufs=NTR)
             st[("tr", key, t, half)] = b_
             w = st[(key, t)][:].bitcast(F32)
             for i in range(4):
                 n = half * 4 + i
                 nc.tensor.transpose(b_[:, i, :], w[:, n * P : (n + 1) * P], id_f[:])
 
-        def s_cp(key, t, half):
-            if half == 0:
-                new(key + "t", t, [P, K], BF16, 2)
-            dst = st[(key + "t", t)][:, half * 1024 : (half + 1) * 1024].bitcast(F32)
+        def cp(t, key, half):
+            dst = new(key + "t", t, [P, K], BF16)[:, half * 1024 : (half + 1) * 1024].bitcast(F32)
             nc.scalar.copy(out=dst.rearrange("p (c r u) -> p c r u", c=2, u=2),
                            in_=st[("tr", key, t, half)][:].rearrange("p (c u) r -> p c r u", c=2))
 
-        def v_q(key, t):
-            codes = new(key + "c", t, [P, D], U32, 2)
-            sc = new(key + "s", t, [P, D], U8, 2)
+        def quant(t, key):
+            codes = new(key + "c", t, [P, D], U32)
+            sc = new(key + "s", t, [P, D], U8)
             nc.vector.quantize_mx(out=codes[:].bitcast(FP8X4), scales=sc[:], in_=st[(key + "t", t)][:])
 
-        def t_mx(key, t):
-            acc = ps.tile([P, D], F32, name="mx", tag="mx")
+        def mx(t, key):
+            acc = ps.tile([P, D], F32, name="mx", tag="mx", bufs=NMX)
             st[("mx", key, t)] = acc
             codes, sc = st[(key + "c", t)], st[(key + "s", t)]
             for c in range(C):
@@ -194,54 +229,53 @@ def tile_linearneuralcdetwoeulersteps_x2_kernel(tc, h0, dx, a_words, a_scales, g
                     out=acc[:], lhsT=codes[:, c * P : (c + 1) * P].bitcast(FP8X4), lhsT_scale=sc[:, c * P : (c + 1) * P],
                     rhs=aw[:, c, :].bitcast(FP4X4), rhs_scale=asc[:, c, :], start=(c == 0), stop=(c == C - 1))
 
-        def v_h1(t):
-            h = new("h1", t, [P, D], F32, 3)
+        def h1_add(t):
+            h = new("h1", t, [P, D], F32)
             nc.vector.tensor_tensor(out=lin(h[:]), in0=perm(st[("mx", "z1", t)][:]), in1=lin(st[("ph", t)][:]), op=ADD)
 
-        def v_z2(t):
-            z = new("z2", t, [P, K], BF16, 2)
-            for c in range(C):
-                nc.vector.scalar_tensor_tensor(out=z[:, c * D : (c + 1) * D], in0=st[("h1", t)][:], scalar=ecol(1, t, c),
-                                               in1=gps(c), op0=MULT, op1=MULT)
-
-        def t_eb(t):
-            eb = ps.tile([P, D], F32, name="eb", tag="eb")
+        def eb_mm(t):
+            eb = ps.tile([P, D], F32, name="eb", tag="eb", bufs=NEB)
             st[("eb", t)] = eb
             nc.tensor.matmul(eb[:], lhsT=st[("m1", t)][:], rhs=b_rep[:], start=True, stop=True)
 
-        def v_w(t):
-            w = new("w", t, [P, D], F32, 2)
+        def w_add(t):
+            w = new("w", t, [P, D], F32)
             nc.vector.tensor_tensor(out=nat(w[:]), in0=unperm(st[("h1", t)][:]), in1=nat(st[("eb", t)][:]), op=ADD)
 
-        def v_out(t):
-            o = new("o", t, [P, D], F32, 3)
+        def out_add(t):
+            o = new("o", t, [P, D], F32)
             nc.vector.tensor_tensor(out=o[:], in0=st[("mx", "z2", t)][:], in1=st[("w", t)][:], op=ADD)
             nc.sync.dma_start(out=out_v[t // G][:, t % G, :], in_=o[:])
 
-        def s_ob(t):
-            ob = new("ob", t, [P, D], BF16, 3)
+        def ob_cp(t):
+            ob = new("ob", t, [P, D], BF16)
             nc.scalar.copy(out=lin(ob[:]), in_=perm(st[("o", t)][:]))
 
-        def t_trp(t):
-            b_ = ps.tile([P, 4, P], F32, name="tr", tag="tr")
+        def p_tr(t):
+            if t % 2 == 0:
+                return
+            b_ = ps.tile([P, 4, P], F32, name="tr", tag="tr", bufs=NTR)
             st[("trp", t)] = b_
             for jj in range(2):
                 w = st[("ob", t - 1 + jj)][:].bitcast(F32)
                 for u in range(2):
                     nc.tensor.transpose(b_[:, 2 * jj + u, :], w[:, u * P : (u + 1) * P], id_f[:])
 
-        def s_cpp(t):
+        def p_out(t):
+            if t % 2 == 0:
+                return
             g = t // G
-            if t % G == 1:
-                new("pt", g, [P, K], BF16, 2)
-            dst = st[("pt", g)][:].bitcast(F32).rearrange("p (q j u) -> p q j u", j=4, u=2)
+            dst = new("pt", g, [P, K], BF16)[:].bitcast(F32).rearrange("p (q j u) -> p q j u", j=4, u=2)
             h = (t % G) // 2
             nc.scalar.copy(out=dst[:, :, 2 * h : 2 * h + 2, :],
                            in_=st[("trp", t)][:].rearrange("p (j u) q -> p q j u", u=2))
 
-        def v_planes(g):
-            codes = new("pc", g, [P, D], U32, 2)
-            sc = new("psc", g, [P, D], U8, 2)
+        def planes(t):
+            if t % 4 != 3:
+                return
+            g = t // G
+            codes = new("pc", g, [P, D], U32)
+            sc = new("psc", g, [P, D], U8)
             nc.vector.quantize_mx(out=codes[:].bitcast(FP8X4), scales=sc[:], in_=st[("pt", g)][:])
             dst = out_1.rearrange("o p m t -> (o p) (m t)")
             nc.sync.dma_start(out=dst[:, g * K : (g + 1) * K].bitcast(I32), in_=codes[:].bitcast(I32))
@@ -250,51 +284,23 @@ def tile_linearneuralcdetwoeulersteps_x2_kernel(tc, h0, dx, a_words, a_scales, g
                 nc.sync.dma_start(out=dst2[4 * q : 4 * q + 4, g * D : (g + 1) * D].bitcast(I32),
                                   in_=sc[32 * q : 32 * q + 4, :].bitcast(I32))
 
-        def ok(t):
-            return 0 <= t < TILES
-
-        for k in range(-2, TILES + 4):
-            if ok(k + 2):
-                g_u(k + 2)
-            if ok(k + 1):
-                s_z1(k + 1)
-                t_p(k + 1)
-                s_p(k + 1)
-            if ok(k - 2):
-                v_q("z2", k - 2)
-                t_mx("z2", k - 2)
-            if ok(k):
-                v_q("z1", k)
-                t_mx("z1", k)
-            if ok(k - 1):
-                v_z2(k - 1)
-                t_tr("z2", k - 1, 0)
-                s_cp("z2", k - 1, 0)
-            if ok(k - 2):
-                v_out(k - 2)
-            if ok(k + 1):
-                t_tr("z1", k + 1, 0)
-                s_cp("z1", k + 1, 0)
-                t_tr("z1", k + 1, 1)
-                s_cp("z1", k + 1, 1)
-            if ok(k + 2):
-                v_z1(k + 2)
-            if ok(k - 1):
-                t_tr("z2", k - 1, 1)
-                s_cp("z2", k - 1, 1)
-                t_eb(k - 1)
-            if ok(k):
-                v_h1(k)
-            if ok(k - 1):
-                v_w(k - 1)
-            if ok(k - 2):
-                s_ob(k - 2)
-                if (k - 2) % 2 == 1:
-                    t_trp(k - 2)
-                    s_cpp(k - 2)
-            if ok(k - 3) and (k - 3) % G == 3:
-                v_planes((k - 3) // G)
-            if ok(k + 2):
-                v_mask(0, k + 2)
-            if ok(k):
-                v_mask(1, k)
+        run = {"m0": (mask, 0), "m1": (mask, 1), "P": (p_mm,), "cP": (p_cp,), "q1": (quant, "z1"), "q2": (quant, "z2"),
+               "mx1": (mx, "z1"), "mx2": (mx, "z2"), "h1": (h1_add,), "eb": (eb_mm,), "w": (w_add,), "out": (out_add,),
+               "ob": (ob_cp,), "trp": (p_tr,), "cpp": (p_out,), "pq": (planes,)}
+        for s in (1, 2):
+            for half, ab in enumerate("ab"):
+                run["tr%d%s" % (s, ab)] = (tr, "z%d" % s, half)
+                run["c%d%s" % (s, ab)] = (cp, "z%d" % s, half)
+        for c in range(C):
+            run["z1%d" % c] = (z1, c)
+            run["u1%d" % c] = (u1, c)
+            run["a1%d" % c] = (a1, c)
+            run["z2%d" % c] = (z2, c)
+            run["u2%d" % c] = (u2, c)
+            run["a2%d" % c] = (a2, c)
+        lo = min(lag for n, lag in SEQ)
+        hi = max(lag for n, lag in SEQ)
+        for k in range(lo, TILES + hi):
+            for n, lag in SEQ:
+                if 0 <= k - lag < TILES:
+                    run[n][0](k - lag, *run[n][1:])

@@ -22,16 +22,13 @@ AX = mybir.AxisListType
 P = 128
 TILES = R // P
 G = 4
-BUFS = {"pt":2,"pc":2,"psc":2,"m0":2,"m1":5,"ph":6,"z1t":5,"z2t":2,"z1c":2,"z1s":2,"z2c":2,"z2s":2,"h1":4,"w":3,"o":3,"z1":5,"z2":2,"ob":5}
-NTR, NMX, NEB = 2, 2, 2
-G1 = ()
-G2 = ()
-G2X = {}
+BUFS = {"mz1":2,"mz2":2,"z1t":3,"z2t":3,"z1c":2,"z1s":2,"z2c":2,"z2s":2,"h1":5,"o":3,"z1":2,"z2":2,"ob":4,"pt":2,"pc":2,"psc":2}
+NTR, NMX, NH, NO = 2, 2, 2, 2
 SEQ = [
-    ("trp", 1), ("q1", -6), ("tr1b", -7), ("q2", -3), ("h1", -5), ("w", -3), ("cP", -10), ("tr2a", -4),
-    ("tr2b", -4), ("c1a", -10), ("out", -2), ("m1", -7), ("eb", -4), ("z12", -9), ("mx1", -6), ("pq", 2),
-    ("cpp", 1), ("c2a", -4), ("z20", -5), ("P", -11), ("z21", -5), ("mx2", -3), ("m0", -12), ("z22", -5),
-    ("z11", -11), ("z10", -11), ("c1b", -7), ("tr1a", -11), ("z23", -5), ("c2b", -4), ("z13", -8), ("ob", -2),
+    ("z11", -5), ("ob", 2), ("mx2", 0), ("trp", 3), ("t2", 1), ("z12", -5), ("cpp", 3), ("tr1a", -5),
+    ("c1a", -5), ("z13", -5), ("q1", -4), ("z21", -2), ("z23", -2), ("e2", 0), ("z22", -2), ("t1", -3),
+    ("tr1b", -5), ("z20", -2), ("c1b", -5), ("mx1", -4), ("tr2b", -2), ("c2b", -2), ("q2", -1), ("tr2a", -2),
+    ("out", 1), ("pq", 3), ("z10", -6), ("p2", 0), ("hc", -3), ("e1", -4), ("c2a", -2), ("p1", -4),
 ]
 
 
@@ -56,7 +53,6 @@ def tile_linearneuralcdetwoeulersteps_x2_kernel(tc, h0, dx, a_words, a_scales, g
     with ExitStack() as ctx:
         keep = ctx.enter_context(tc.tile_pool(name="keep", bufs=1))
         work = ctx.enter_context(tc.tile_pool(name="work", bufs=3))
-        psk = ctx.enter_context(tc.psum_pool(name="psk", bufs=1))
         ps = ctx.enter_context(tc.psum_pool(name="ps", bufs=2))
         ctx.enter_context(tc.manual_schedule())
 
@@ -65,36 +61,32 @@ def tile_linearneuralcdetwoeulersteps_x2_kernel(tc, h0, dx, a_words, a_scales, g
         dx_v = dx.rearrange("s (g p j) c -> s p g (j c)", g=4, j=4)
 
         h_in = [keep.tile([P, G, D], BF16, name="h_in%d" % g, align_bytes=64) for g in range(4)]
+        h_p = [keep.tile([P, G, D], BF16, name="h_p%d" % g, align_bytes=64) for g in range(4)]
         e_bf = keep.tile([P, 2, 4, 16], BF16, name="e_bf")
         e_f = keep.tile([P, 128], F32, name="e_f")
         e_t = keep.tile([P, 128], BF16, name="e_t")
-        gain_row = keep.tile([P, K], BF16, name="gain_row", align_bytes=64)
-        ones_row = keep.tile([P, P], BF16, name="ones_row", align_bytes=64)
-        gain_f = keep.tile([P, K], F32, name="gain_f", align_bytes=64)
-        gain_sb = keep.tile([P, K], BF16, name="gain_sb", align_bytes=64)
-        b_rep = keep.tile([P, D], BF16, name="b_rep", align_bytes=64)
+        gain_n = keep.tile([P, C, D], BF16, name="gain_n", align_bytes=64)
+        gain_p = keep.tile([P, C, D], BF16, name="gain_p", align_bytes=64)
+        b_n = keep.tile([P, D], BF16, name="b_n", align_bytes=64)
+        b_p = keep.tile([P, D], BF16, name="b_p", align_bytes=64)
         aw = keep.tile([P, 4, 2 * D], U8, name="aw", align_bytes=64)
         asc = keep.tile([P, 4, D], U8, name="asc", align_bytes=64)
         id_f = keep.tile([P, P], F32, name="id_f", align_bytes=64)
         id_b = keep.tile([P, P], BF16, name="id_b", align_bytes=64)
         sel = keep.tile([P, 32], F32, name="sel")
-        gain_ps = [psk.tile([P, 1024], BF16, name="gain_ps%d" % i) for i in range(2)]
+        mask = keep.tile([P, 32, P], BF16, name="mask", align_bytes=64)
 
-        nc.vector.memset(gain_row[:], 0.0)
-        nc.vector.memset(ones_row[:], 0.0)
-        nc.vector.memset(ones_row[0:1, :], 1.0)
-        nc.vector.memset(asc[:].rearrange("p g n -> p (g n)").bitcast(I32), 0)
         make_identity(nc, id_f[:])
-
-        nc.scalar.dma_start(out=gain_row[0:1, :], in_=gain.rearrange("(o c) d -> o (c d)", o=1))
         nc.sync.dma_start(out=h_in[0][:, 0:1, :], in_=h0_v[0][:, 0:1, :])
         for s in range(2):
-            nc.sync.dma_start(out=e_bf[:, s], in_=dx_v[s])
+            nc.scalar.dma_start(out=e_bf[:, s], in_=dx_v[s])
+        for c in range(C):
+            nc.sync.dma_start(out=gain_n[:, c, :], in_=gain[c].partition_broadcast(P))
+        nc.vector.memset(asc[:].rearrange("p g n -> p (g n)").bitcast(I32), 0)
         nc.sync.dma_start(out=h_in[0][:, 1:4, :], in_=h0_v[0][:, 1:4, :])
         for c in range(C):
-            nc.scalar.dma_start(out=b_rep[c:P:4, :], in_=b[c : c + 1, :].to_broadcast([32, D]))
-        nc.sync.dma_start(
-            out=aw[:].bitcast(I32), in_=a_words.bitcast(I32).rearrange("g p n -> p g n"))
+            nc.scalar.dma_start(out=b_n[c:P:4, :], in_=b[c : c + 1, :].to_broadcast([32, D]))
+        nc.sync.dma_start(out=aw[:].bitcast(I32), in_=a_words.bitcast(I32).rearrange("g p n -> p g n"))
         for q in range(4):
             nc.sync.dma_start(
                 out=asc[32 * q : 32 * q + 4].bitcast(I32),
@@ -102,22 +94,27 @@ def tile_linearneuralcdetwoeulersteps_x2_kernel(tc, h0, dx, a_words, a_scales, g
         for g in range(1, 4):
             nc.sync.dma_start(out=h_in[g][:], in_=h0_v[g])
 
+        def words(ap):
+            return ap.bitcast(F32)
+
+        def h_perm(g, j0, j1):
+            nc.scalar.copy(out=words(h_p[g][:, j0:j1, :]).rearrange("k j (u p) -> k j u p", u=2),
+                           in_=words(h_in[g][:, j0:j1, :]).rearrange("k j (p u) -> k j u p", u=2))
+
         nc.vector.tensor_copy(out=id_b[:], in_=id_f[:])
         nc.vector.tensor_reduce(out=sel[:], in_=id_f[:].rearrange("k (i c) -> k i c", c=4), op=ADD, axis=AX.X)
+        e_all = e_bf[:].rearrange("p s g x -> p (s g x)")
+        nc.scalar.activation(out=e_f[:], in_=e_all, func=COPY)
+        h_perm(0, 0, 1)
+        et_ps = ps.tile([P, P], BF16, name="et_ps", tag="tr", bufs=NTR)
+        nc.tensor.transpose(et_ps[:], e_all, id_b[:])
         for c in range(C):
-            nc.tensor.matmul(lin(gain_ps[c // 2][:, (c % 2) * D : (c % 2 + 1) * D]), lhsT=ones_row[:],
-                             rhs=perm(gain_row[:, c * D : (c + 1) * D]), start=True, stop=True)
-        nc.scalar.activation(out=e_f[:], in_=e_bf[:].rearrange("p s g x -> p (s g x)"), func=COPY)
-        et_ps = ps.tile([P, P], BF16, name="et_ps", tag="tr")
-        nc.tensor.transpose(et_ps[:], e_bf[:].rearrange("p s g x -> p (s g x)"), id_b[:])
-        nc.vector.tensor_copy(out=e_t[:], in_=et_ps[:])
-        for c in range(C):
-            if c in G1:
-                nc.scalar.copy(out=nat(gain_sb[:, c * D : (c + 1) * D]),
-                               in_=unperm(gain_ps[c // 2][:, (c % 2) * D : (c % 2 + 1) * D]))
-        for c in range(C):
-            if c in G2:
-                nc.scalar.copy(out=gain_f[:, c * D : (c + 1) * D], in_=gain_ps[c // 2][:, (c % 2) * D : (c % 2 + 1) * D])
+            nc.vector.tensor_copy(out=words(gain_p[:, c, :]).rearrange("k (u p) -> k u p", u=2),
+                                  in_=words(gain_n[:, c, :]).rearrange("k (p u) -> k u p", u=2))
+        nc.scalar.copy(out=e_t[:], in_=et_ps[:])
+        h_perm(0, 1, 4)
+        nc.scalar.copy(out=words(b_p[:]).rearrange("k (u p) -> k u p", u=2),
+                       in_=words(b_n[:]).rearrange("k (p u) -> k u p", u=2))
 
         st = {}
 
@@ -127,91 +124,35 @@ def tile_linearneuralcdetwoeulersteps_x2_kernel(tc, h0, dx, a_words, a_scales, g
                 st[(key, t)] = x
             return st[(key, t)]
 
-        def hrow(t):
-            return h_in[t // G][:, t % G, :]
-
         def ecol(s, t, c):
             i = (s * TILES + t) * 4 + c
             return e_f[:, i : i + 1]
 
-        def gps(c):
-            return gain_ps[c // 2][:, (c % 2) * D : (c % 2 + 1) * D]
-
-        def g1(t):
-            return () if t == 0 else G1
-
-        def g2(t):
-            return G2X.get(t, G2)
-
         def z1(t, c):
-            if c in g1(t):
-                return
+            if c == 0:
+                if t % G == 1 and t // G < 3:
+                    h_perm(t // G + 1, 0, 4)
+                for i in (t, TILES + t):
+                    nc.scalar.activation(out=mask[:, i, :], in_=e_t[:], func=COPY, scale=sel[:, i : i + 1])
             z = new("z1", t, [P, K], BF16)
-            for u in range(2):
-                nc.vector.scalar_tensor_tensor(
-                    out=z[:, c * D + 256 * u : c * D + 256 * (u + 1)].rearrange("k (p e) -> k p e", e=2),
-                    in0=perm(hrow(t))[:, u], scalar=ecol(0, t, c),
-                    in1=gps(c)[:, 256 * u : 256 * (u + 1)].rearrange("k (p e) -> k p e", e=2), op0=MULT, op1=MULT)
-
-        def u1(t, c):
-            if c in g1(t):
-                u = new("u1%d" % c, t, [P, D], F32)
-                nc.gpsimd.tensor_tensor(out=u[:], in0=hrow(t), in1=gain_sb[:, c * D : (c + 1) * D], op=MULT)
-
-        def a1(t, c):
-            if c in g1(t):
-                z = new("z1", t, [P, K], BF16)
-                nc.scalar.activation(out=lin(z[:, c * D : (c + 1) * D]), in_=perm(st[("u1%d" % c, t)][:]), func=COPY,
-                                     scale=ecol(0, t, c))
+            nc.vector.scalar_tensor_tensor(out=z[:, c * D : (c + 1) * D], in0=h_p[t // G][:, t % G, :],
+                                           scalar=ecol(0, t, c), in1=gain_p[:, c, :], op0=MULT, op1=MULT)
 
         def z2(t, c):
-            if c in g2(t):
-                return
             z = new("z2", t, [P, K], BF16)
-            nc.vector.scalar_tensor_tensor(out=z[:, c * D : (c + 1) * D], in0=st[("h1", t)][:], scalar=ecol(1, t, c),
-                                           in1=gps(c), op0=MULT, op1=MULT)
-
-        def u2(t, c):
-            if c in g2(t):
-                u = new("u2%d" % c, t, [P, D], F32)
-                nc.gpsimd.tensor_tensor(out=u[:], in0=st[("h1", t)][:], in1=gain_f[:, c * D : (c + 1) * D], op=MULT)
-
-        def a2(t, c):
-            if c in g2(t):
-                z = new("z2", t, [P, K], BF16)
-                nc.scalar.activation(out=z[:, c * D : (c + 1) * D], in_=st[("u2%d" % c, t)][:], func=COPY,
-                                     scale=ecol(1, t, c))
-
-        def mask(t, s):
-            m = new("m%d" % s, t, [P, P], BF16)
-            i = s * TILES + t
-            nc.vector.tensor_scalar(out=m[:], in0=e_t[:], scalar1=sel[:, i : i + 1], scalar2=None, op0=MULT)
-
-        def p_mm(t):
-            eb = ps.tile([P, D], F32, name="eb", tag="eb", bufs=NEB)
-            st[("p", t)] = eb
-            nc.tensor.matmul(eb[:], lhsT=st[("m0", t)][:], rhs=b_rep[:], start=True, stop=(t == 0))
-            if t > 0:
-                nc.tensor.matmul(eb[:], lhsT=id_b[:], rhs=hrow(t), start=False, stop=True)
-
-        def p_cp(t):
-            p = new("ph", t, [P, D], F32)
-            src = st[("p", t)]
-            if t == 0:
-                nc.vector.tensor_tensor(out=lin(p[:]), in0=perm(src[:]), in1=perm(hrow(t)), op=ADD)
-            else:
-                nc.scalar.copy(out=lin(p[:]), in_=perm(src[:]))
+            nc.vector.scalar_tensor_tensor(out=z[:, c * D : (c + 1) * D], in0=st[("H", t)][:], scalar=ecol(1, t, c),
+                                           in1=gain_p[:, c, :], op0=MULT, op1=MULT)
 
         def tr(t, key, half):
             b_ = ps.tile([P, 4, P], F32, name="tr", tag="tr", bufs=NTR)
             st[("tr", key, t, half)] = b_
-            w = st[(key, t)][:].bitcast(F32)
+            w = words(st[(key, t)][:])
             for i in range(4):
                 n = half * 4 + i
                 nc.tensor.transpose(b_[:, i, :], w[:, n * P : (n + 1) * P], id_f[:])
 
         def cp(t, key, half):
-            dst = new(key + "t", t, [P, K], BF16)[:, half * 1024 : (half + 1) * 1024].bitcast(F32)
+            dst = words(new(key + "t", t, [P, K], BF16)[:, half * 1024 : (half + 1) * 1024])
             nc.scalar.copy(out=dst.rearrange("p (c r u) -> p c r u", c=2, u=2),
                            in_=st[("tr", key, t, half)][:].rearrange("p (c u) r -> p c r u", c=2))
 
@@ -221,30 +162,52 @@ def tile_linearneuralcdetwoeulersteps_x2_kernel(tc, h0, dx, a_words, a_scales, g
             nc.vector.quantize_mx(out=codes[:].bitcast(FP8X4), scales=sc[:], in_=st[(key + "t", t)][:])
 
         def mx(t, key):
-            acc = ps.tile([P, D], F32, name="mx", tag="mx", bufs=NMX)
+            acc = ps.tile([P, 4, P], F32, name="mx", tag="mx", bufs=NMX)
             st[("mx", key, t)] = acc
             codes, sc = st[(key + "c", t)], st[(key + "s", t)]
-            for c in range(C):
-                nc.tensor.matmul_mx(
-                    out=acc[:], lhsT=codes[:, c * P : (c + 1) * P].bitcast(FP8X4), lhsT_scale=sc[:, c * P : (c + 1) * P],
-                    rhs=aw[:, c, :].bitcast(FP4X4), rhs_scale=asc[:, c, :], start=(c == 0), stop=(c == C - 1))
+            for m in range(4):
+                for c in range(C):
+                    nc.tensor.matmul_mx(
+                        out=acc[:, m, :], lhsT=aw[:, c, 256 * m : 256 * (m + 1)].bitcast(FP4X4),
+                        lhsT_scale=asc[:, c, P * m : P * (m + 1)],
+                        rhs=codes[:, c * P : (c + 1) * P].bitcast(FP8X4), rhs_scale=sc[:, c * P : (c + 1) * P],
+                        start=(c == 0), stop=(c == C - 1))
 
-        def h1_add(t):
+        def evac(t, key):
+            m = new("m" + key, t, [P, 4, P], F32)
+            nc.scalar.copy(out=m[:], in_=st[("mx", key, t)][:])
+
+        def p1(t):
+            h = ps.tile([P, D], F32, name="H", tag="H", bufs=NH)
+            st[("H", t)] = h
+            nc.tensor.matmul(h[:], lhsT=mask[:, t, :], rhs=b_p[:], start=True, stop=False)
+            nc.tensor.matmul(h[:], lhsT=id_b[:], rhs=h_p[t // G][:, t % G, :], start=False, stop=False)
+
+        def t1(t):
+            h = st[("H", t)][:].rearrange("k (u p e) -> k p u e", u=2, e=2)
+            for m in range(4):
+                nc.tensor.matmul(h[:, 32 * m : 32 * (m + 1)], lhsT=st[("mz1", t)][:, m, :],
+                                 rhs=id_f[:].rearrange("k (p u e) -> k p u e", u=2, e=2), is_transpose=True,
+                                 start=False, stop=(m == 3))
+
+        def h_cp(t):
             h = new("h1", t, [P, D], F32)
-            nc.vector.tensor_tensor(out=lin(h[:]), in0=perm(st[("mx", "z1", t)][:]), in1=lin(st[("ph", t)][:]), op=ADD)
+            nc.scalar.copy(out=nat(h[:]), in_=unperm(st[("H", t)][:]))
 
-        def eb_mm(t):
-            eb = ps.tile([P, D], F32, name="eb", tag="eb", bufs=NEB)
-            st[("eb", t)] = eb
-            nc.tensor.matmul(eb[:], lhsT=st[("m1", t)][:], rhs=b_rep[:], start=True, stop=True)
+        def p2(t):
+            o = ps.tile([P, D], F32, name="O", tag="O", bufs=NO)
+            st[("O", t)] = o
+            nc.tensor.matmul(o[:], lhsT=mask[:, TILES + t, :], rhs=b_n[:], start=True, stop=False)
 
-        def w_add(t):
-            w = new("w", t, [P, D], F32)
-            nc.vector.tensor_tensor(out=nat(w[:]), in0=unperm(st[("h1", t)][:]), in1=nat(st[("eb", t)][:]), op=ADD)
+        def t2(t):
+            o = st[("O", t)]
+            for m in range(4):
+                nc.tensor.matmul(o[:, P * m : P * (m + 1)], lhsT=st[("mz2", t)][:, m, :], rhs=id_f[:], is_transpose=True,
+                                 start=False, stop=(m == 3))
 
         def out_add(t):
             o = new("o", t, [P, D], F32)
-            nc.vector.tensor_tensor(out=o[:], in0=st[("mx", "z2", t)][:], in1=st[("w", t)][:], op=ADD)
+            nc.vector.tensor_tensor(out=o[:], in0=st[("O", t)][:], in1=st[("h1", t)][:], op=ADD)
             nc.sync.dma_start(out=out_v[t // G][:, t % G, :], in_=o[:])
 
         def ob_cp(t):
@@ -257,7 +220,7 @@ def tile_linearneuralcdetwoeulersteps_x2_kernel(tc, h0, dx, a_words, a_scales, g
             b_ = ps.tile([P, 4, P], F32, name="tr", tag="tr", bufs=NTR)
             st[("trp", t)] = b_
             for jj in range(2):
-                w = st[("ob", t - 1 + jj)][:].bitcast(F32)
+                w = words(st[("ob", t - 1 + jj)][:])
                 for u in range(2):
                     nc.tensor.transpose(b_[:, 2 * jj + u, :], w[:, u * P : (u + 1) * P], id_f[:])
 
@@ -265,13 +228,13 @@ def tile_linearneuralcdetwoeulersteps_x2_kernel(tc, h0, dx, a_words, a_scales, g
             if t % 2 == 0:
                 return
             g = t // G
-            dst = new("pt", g, [P, K], BF16)[:].bitcast(F32).rearrange("p (q j u) -> p q j u", j=4, u=2)
+            dst = words(new("pt", g, [P, K], BF16)[:]).rearrange("p (q j u) -> p q j u", j=4, u=2)
             h = (t % G) // 2
             nc.scalar.copy(out=dst[:, :, 2 * h : 2 * h + 2, :],
                            in_=st[("trp", t)][:].rearrange("p (j u) q -> p q j u", u=2))
 
         def planes(t):
-            if t % 4 != 3:
+            if t % G != 3:
                 return
             g = t // G
             codes = new("pc", g, [P, D], U32)
@@ -284,8 +247,8 @@ def tile_linearneuralcdetwoeulersteps_x2_kernel(tc, h0, dx, a_words, a_scales, g
                 nc.sync.dma_start(out=dst2[4 * q : 4 * q + 4, g * D : (g + 1) * D].bitcast(I32),
                                   in_=sc[32 * q : 32 * q + 4, :].bitcast(I32))
 
-        run = {"m0": (mask, 0), "m1": (mask, 1), "P": (p_mm,), "cP": (p_cp,), "q1": (quant, "z1"), "q2": (quant, "z2"),
-               "mx1": (mx, "z1"), "mx2": (mx, "z2"), "h1": (h1_add,), "eb": (eb_mm,), "w": (w_add,), "out": (out_add,),
+        run = {"q1": (quant, "z1"), "q2": (quant, "z2"), "mx1": (mx, "z1"), "mx2": (mx, "z2"), "e1": (evac, "z1"),
+               "e2": (evac, "z2"), "p1": (p1,), "p2": (p2,), "t1": (t1,), "t2": (t2,), "hc": (h_cp,), "out": (out_add,),
                "ob": (ob_cp,), "trp": (p_tr,), "cpp": (p_out,), "pq": (planes,)}
         for s in (1, 2):
             for half, ab in enumerate("ab"):
@@ -293,11 +256,7 @@ def tile_linearneuralcdetwoeulersteps_x2_kernel(tc, h0, dx, a_words, a_scales, g
                 run["c%d%s" % (s, ab)] = (cp, "z%d" % s, half)
         for c in range(C):
             run["z1%d" % c] = (z1, c)
-            run["u1%d" % c] = (u1, c)
-            run["a1%d" % c] = (a1, c)
             run["z2%d" % c] = (z2, c)
-            run["u2%d" % c] = (u2, c)
-            run["a2%d" % c] = (a2, c)
         lo = min(lag for n, lag in SEQ)
         hi = max(lag for n, lag in SEQ)
         for k in range(lo, TILES + hi):

from contextlib import ExitStack

import concourse.mybir as mybir
from concourse.masks import make_identity

R, C, D = 2048, 4, 512
K = C * D
FLOPS = 2 * 2 * R * K * D

F32 = mybir.dt.float32
BF16 = mybir.dt.bfloat16
I32 = mybir.dt.int32
U32 = mybir.dt.uint32
U8 = mybir.dt.uint8
FP8X4 = mybir.dt.float8_e4m3fn_x4
FP4X4 = mybir.dt.float4_e2m1fn_x4
MULT = mybir.AluOpType.mult
ADD = mybir.AluOpType.add
COPY = mybir.ActivationFunctionType.Copy
AX = mybir.AxisListType

P = 128
TILES = R // P
G = 4
BUFS = {"mz1":2,"mz2":2,"z1t":3,"z2t":3,"z1c":2,"z1s":2,"z2c":2,"z2s":2,"h1":5,"o":3,"z1":2,"z2":2,"ob":4,"pt":2,"pc":2,"psc":2}
NTR, NMX, NH, NO = 2, 2, 2, 2
SEQ = [
    ("z11", -5), ("ob", 2), ("mx2", 0), ("trp", 3), ("t2", 1), ("z12", -5), ("cpp", 3), ("tr1a", -5),
    ("c1a", -5), ("z13", -5), ("q1", -4), ("z21", -2), ("z23", -2), ("e2", 0), ("z22", -2), ("t1", -3),
    ("tr1b", -5), ("z20", -2), ("c1b", -5), ("mx1", -4), ("tr2b", -2), ("c2b", -2), ("q2", -1), ("tr2a", -2),
    ("out", 1), ("pq", 3), ("z10", -6), ("p2", 0), ("hc", -3), ("e1", -4), ("c2a", -2), ("p1", -4),
]


def perm(ap):
    return ap.rearrange("k (p u e) -> k u p e", u=2, e=2)


def lin(ap):
    return ap.rearrange("k (u p e) -> k u p e", u=2, e=2)


def unperm(ap):
    return ap.rearrange("k (u p e) -> k p u e", u=2, e=2)


def nat(ap):
    return ap.rearrange("k (p u e) -> k p u e", u=2, e=2)


def tile_linearneuralcdetwoeulersteps_x2_kernel(tc, h0, dx, a_words, a_scales, gain, b, out_0, out_1, out_2):
    nc = tc.nc
    with ExitStack() as ctx:
        keep = ctx.enter_context(tc.tile_pool(name="keep", bufs=1))
        work = ctx.enter_context(tc.tile_pool(name="work", bufs=3))
        ps = ctx.enter_context(tc.psum_pool(name="ps", bufs=2))
        ctx.enter_context(tc.manual_schedule())

        h0_v = h0.rearrange("(g p j) d -> g p j d", g=4, j=4)
        out_v = out_0.rearrange("(g p j) d -> g p j d", g=4, j=4)
        dx_v = dx.rearrange("s (g p j) c -> s p g (j c)", g=4, j=4)

        h_in = [keep.tile([P, G, D], BF16, name="h_in%d" % g, align_bytes=64) for g in range(4)]
        h_p = [keep.tile([P, G, D], BF16, name="h_p%d" % g, align_bytes=64) for g in range(4)]
        e_bf = keep.tile([P, 2, 4, 16], BF16, name="e_bf")
        e_f = keep.tile([P, 128], F32, name="e_f")
        e_t = keep.tile([P, 128], BF16, name="e_t")
        gain_n = keep.tile([P, C, D], BF16, name="gain_n", align_bytes=64)
        gain_p = keep.tile([P, C, D], BF16, name="gain_p", align_bytes=64)
        b_n = keep.tile([P, D], BF16, name="b_n", align_bytes=64)
        b_p = keep.tile([P, D], BF16, name="b_p", align_bytes=64)
        aw = keep.tile([P, 4, 2 * D], U8, name="aw", align_bytes=64)
        asc = keep.tile([P, 4, D], U8, name="asc", align_bytes=64)
        id_f = keep.tile([P, P], F32, name="id_f", align_bytes=64)
        id_b = keep.tile([P, P], BF16, name="id_b", align_bytes=64)
        sel = keep.tile([P, 32], F32, name="sel")
        mask = keep.tile([P, 32, P], BF16, name="mask", align_bytes=64)

        make_identity(nc, id_f[:])
        nc.sync.dma_start(out=h_in[0][:, 0:1, :], in_=h0_v[0][:, 0:1, :])
        for s in range(2):
            nc.scalar.dma_start(out=e_bf[:, s], in_=dx_v[s])
        for c in range(C):
            nc.sync.dma_start(out=gain_n[:, c, :], in_=gain[c].partition_broadcast(P))
        nc.vector.memset(asc[:].rearrange("p g n -> p (g n)").bitcast(I32), 0)
        nc.sync.dma_start(out=h_in[0][:, 1:4, :], in_=h0_v[0][:, 1:4, :])
        for c in range(C):
            nc.scalar.dma_start(out=b_n[c:P:4, :], in_=b[c : c + 1, :].to_broadcast([32, D]))
        nc.sync.dma_start(out=aw[:].bitcast(I32), in_=a_words.bitcast(I32).rearrange("g p n -> p g n"))
        for q in range(4):
            nc.sync.dma_start(
                out=asc[32 * q : 32 * q + 4].bitcast(I32),
                in_=a_scales.bitcast(I32).rearrange("g q n -> q g n")[4 * q : 4 * q + 4])
        for g in range(1, 4):
            nc.sync.dma_start(out=h_in[g][:], in_=h0_v[g])

        def words(ap):
            return ap.bitcast(F32)

        def h_perm(g, j0, j1):
            nc.scalar.copy(out=words(h_p[g][:, j0:j1, :]).rearrange("k j (u p) -> k j u p", u=2),
                           in_=words(h_in[g][:, j0:j1, :]).rearrange("k j (p u) -> k j u p", u=2))

        nc.vector.tensor_copy(out=id_b[:], in_=id_f[:])
        nc.vector.tensor_reduce(out=sel[:], in_=id_f[:].rearrange("k (i c) -> k i c", c=4), op=ADD, axis=AX.X)
        e_all = e_bf[:].rearrange("p s g x -> p (s g x)")
        nc.scalar.activation(out=e_f[:], in_=e_all, func=COPY)
        h_perm(0, 0, 1)
        et_ps = ps.tile([P, P], BF16, name="et_ps", tag="tr", bufs=NTR)
        nc.tensor.transpose(et_ps[:], e_all, id_b[:])
        for c in range(C):
            nc.vector.tensor_copy(out=words(gain_p[:, c, :]).rearrange("k (u p) -> k u p", u=2),
                                  in_=words(gain_n[:, c, :]).rearrange("k (p u) -> k u p", u=2))
        nc.scalar.copy(out=e_t[:], in_=et_ps[:])
        h_perm(0, 1, 4)
        nc.scalar.copy(out=words(b_p[:]).rearrange("k (u p) -> k u p", u=2),
                       in_=words(b_n[:]).rearrange("k (p u) -> k u p", u=2))

        st = {}

        def new(key, t, shape, dt):
            if (key, t) not in st:
                x = work.tile(shape, dt, name=key, bufs=BUFS[key], align_bytes=64)
                st[(key, t)] = x
            return st[(key, t)]

        def ecol(s, t, c):
            i = (s * TILES + t) * 4 + c
            return e_f[:, i : i + 1]

        def z1(t, c):
            if c == 0:
                if t % G == 1 and t // G < 3:
                    h_perm(t // G + 1, 0, 4)
                for i in (t, TILES + t):
                    nc.scalar.activation(out=mask[:, i, :], in_=e_t[:], func=COPY, scale=sel[:, i : i + 1])
            z = new("z1", t, [P, K], BF16)
            nc.vector.scalar_tensor_tensor(out=z[:, c * D : (c + 1) * D], in0=h_p[t // G][:, t % G, :],
                                           scalar=ecol(0, t, c), in1=gain_p[:, c, :], op0=MULT, op1=MULT)

        def z2(t, c):
            z = new("z2", t, [P, K], BF16)
            nc.vector.scalar_tensor_tensor(out=z[:, c * D : (c + 1) * D], in0=st[("H", t)][:], scalar=ecol(1, t, c),
                                           in1=gain_p[:, c, :], op0=MULT, op1=MULT)

        def tr(t, key, half):
            b_ = ps.tile([P, 4, P], F32, name="tr", tag="tr", bufs=NTR)
            st[("tr", key, t, half)] = b_
            w = words(st[(key, t)][:])
            for i in range(4):
                n = half * 4 + i
                nc.tensor.transpose(b_[:, i, :], w[:, n * P : (n + 1) * P], id_f[:])

        def cp(t, key, half):
            dst = words(new(key + "t", t, [P, K], BF16)[:, half * 1024 : (half + 1) * 1024])
            nc.scalar.copy(out=dst.rearrange("p (c r u) -> p c r u", c=2, u=2),
                           in_=st[("tr", key, t, half)][:].rearrange("p (c u) r -> p c r u", c=2))

        def quant(t, key):
            codes = new(key + "c", t, [P, D], U32)
            sc = new(key + "s", t, [P, D], U8)
            nc.vector.quantize_mx(out=codes[:].bitcast(FP8X4), scales=sc[:], in_=st[(key + "t", t)][:])

        def mx(t, key):
            acc = ps.tile([P, 4, P], F32, name="mx", tag="mx", bufs=NMX)
            st[("mx", key, t)] = acc
            codes, sc = st[(key + "c", t)], st[(key + "s", t)]
            for m in range(4):
                for c in range(C):
                    nc.tensor.matmul_mx(
                        out=acc[:, m, :], lhsT=aw[:, c, 256 * m : 256 * (m + 1)].bitcast(FP4X4),
                        lhsT_scale=asc[:, c, P * m : P * (m + 1)],
                        rhs=codes[:, c * P : (c + 1) * P].bitcast(FP8X4), rhs_scale=sc[:, c * P : (c + 1) * P],
                        start=(c == 0), stop=(c == C - 1))

        def evac(t, key):
            m = new("m" + key, t, [P, 4, P], F32)
            nc.scalar.copy(out=m[:], in_=st[("mx", key, t)][:])

        def p1(t):
            h = ps.tile([P, D], F32, name="H", tag="H", bufs=NH)
            st[("H", t)] = h
            nc.tensor.matmul(h[:], lhsT=mask[:, t, :], rhs=b_p[:], start=True, stop=False)
            nc.tensor.matmul(h[:], lhsT=id_b[:], rhs=h_p[t // G][:, t % G, :], start=False, stop=False)

        def t1(t):
            h = st[("H", t)][:].rearrange("k (u p e) -> k p u e", u=2, e=2)
            for m in range(4):
                nc.tensor.matmul(h[:, 32 * m : 32 * (m + 1)], lhsT=st[("mz1", t)][:, m, :],
                                 rhs=id_f[:].rearrange("k (p u e) -> k p u e", u=2, e=2), is_transpose=True,
                                 start=False, stop=(m == 3))

        def h_cp(t):
            h = new("h1", t, [P, D], F32)
            nc.scalar.copy(out=nat(h[:]), in_=unperm(st[("H", t)][:]))

        def p2(t):
            o = ps.tile([P, D], F32, name="O", tag="O", bufs=NO)
            st[("O", t)] = o
            nc.tensor.matmul(o[:], lhsT=mask[:, TILES + t, :], rhs=b_n[:], start=True, stop=False)

        def t2(t):
            o = st[("O", t)]
            for m in range(4):
                nc.tensor.matmul(o[:, P * m : P * (m + 1)], lhsT=st[("mz2", t)][:, m, :], rhs=id_f[:], is_transpose=True,
                                 start=False, stop=(m == 3))

        def out_add(t):
            o = new("o", t, [P, D], F32)
            nc.vector.tensor_tensor(out=o[:], in0=st[("O", t)][:], in1=st[("h1", t)][:], op=ADD)
            nc.sync.dma_start(out=out_v[t // G][:, t % G, :], in_=o[:])

        def ob_cp(t):
            ob = new("ob", t, [P, D], BF16)
            nc.scalar.copy(out=lin(ob[:]), in_=perm(st[("o", t)][:]))

        def p_tr(t):
            if t % 2 == 0:
                return
            b_ = ps.tile([P, 4, P], F32, name="tr", tag="tr", bufs=NTR)
            st[("trp", t)] = b_
            for jj in range(2):
                w = words(st[("ob", t - 1 + jj)][:])
                for u in range(2):
                    nc.tensor.transpose(b_[:, 2 * jj + u, :], w[:, u * P : (u + 1) * P], id_f[:])

        def p_out(t):
            if t % 2 == 0:
                return
            g = t // G
            dst = words(new("pt", g, [P, K], BF16)[:]).rearrange("p (q j u) -> p q j u", j=4, u=2)
            h = (t % G) // 2
            nc.scalar.copy(out=dst[:, :, 2 * h : 2 * h + 2, :],
                           in_=st[("trp", t)][:].rearrange("p (j u) q -> p q j u", u=2))

        def planes(t):
            if t % G != 3:
                return
            g = t // G
            codes = new("pc", g, [P, D], U32)
            sc = new("psc", g, [P, D], U8)
            nc.vector.quantize_mx(out=codes[:].bitcast(FP8X4), scales=sc[:], in_=st[("pt", g)][:])
            dst = out_1.rearrange("o p m t -> (o p) (m t)")
            nc.sync.dma_start(out=dst[:, g * K : (g + 1) * K].bitcast(I32), in_=codes[:].bitcast(I32))
            dst2 = out_2.rearrange("o q m -> (o q) m")
            for q in range(4):
                nc.sync.dma_start(out=dst2[4 * q : 4 * q + 4, g * D : (g + 1) * D].bitcast(I32),
                                  in_=sc[32 * q : 32 * q + 4, :].bitcast(I32))

        run = {"q1": (quant, "z1"), "q2": (quant, "z2"), "mx1": (mx, "z1"), "mx2": (mx, "z2"), "e1": (evac, "z1"),
               "e2": (evac, "z2"), "p1": (p1,), "p2": (p2,), "t1": (t1,), "t2": (t2,), "hc": (h_cp,), "out": (out_add,),
               "ob": (ob_cp,), "trp": (p_tr,), "cpp": (p_out,), "pq": (planes,)}
        for s in (1, 2):
            for half, ab in enumerate("ab"):
                run["tr%d%s" % (s, ab)] = (tr, "z%d" % s, half)
                run["c%d%s" % (s, ab)] = (cp, "z%d" % s, half)
        for c in range(C):
            run["z1%d" % c] = (z1, c)
            run["z2%d" % c] = (z2, c)
        lo = min(lag for n, lag in SEQ)
        hi = max(lag for n, lag in SEQ)
        for k in range(lo, TILES + hi):
            for n, lag in SEQ:
                if 0 <= k - lag < TILES:
                    run[n][0](k - lag, *run[n][1:])
